import numpy as np
import ml_dtypes


def mxq(x, axis, fmt="e4m3"):
    dtype, down = {"e4m3": (ml_dtypes.float8_e4m3fn, 7), "e5m2": (ml_dtypes.float8_e5m2, 14)}[fmt]
    v = np.moveaxis(np.asarray(x, np.float32).astype(ml_dtypes.bfloat16).astype(np.float64), axis, -1)
    blocks = v.reshape(v.shape[:-1] + (-1, 32))
    amax = np.abs(blocks).max(-1, keepdims=True)
    byte = np.maximum(np.where(amax > 0, np.frexp(amax)[1] - 1 + 127, 0) - down, 1)
    scale = np.exp2(byte - 127.0)
    codes = (blocks / scale).astype(np.float32).astype(dtype).astype(np.float64)
    return np.moveaxis((codes * scale).reshape(v.shape), -1, axis)


WIDE = False


def mx_kscale(k):
    if not WIDE:
        return np.ones(k)
    levels = np.array([10, -10, 5, -5, 0])
    if k % 512:
        return np.exp2(np.random.permutation(np.resize(levels, k // 32))).repeat(32)
    a = np.empty((k // 512, 16))
    for p in range(k // 512):
        a[p, :8] = np.random.permutation(np.resize(levels, 8))
        for g in range(8):
            far = levels[np.abs(levels - a[p, g]) >= 10]
            a[p, g + 8] = far[np.random.randint(len(far))]
    return np.exp2(a.ravel()).repeat(32)


def f64(x):
    return np.asarray(x).astype(np.float64)


def striped(idx):
    return np.tile(np.asarray(idx).reshape(-1, 16).T, (8, 1)).astype(np.uint16)


def unstriped(offs):
    return offs[:16].T.reshape(-1).astype(np.int64)


E2M1 = np.array([0.0, 0.5, 1.0, 1.5, 2.0, 3.0, 4.0, 6.0, -0.0, -0.5, -1.0, -1.5, -2.0, -3.0, -4.0, -6.0])


def pack_weight(w, fmt):
    k, n = w.shape
    w = f64(np.asarray(w, np.float32).astype(ml_dtypes.bfloat16)).reshape(k // 32, 32, n)
    amax = np.abs(w).max(1)
    if fmt == "e4m3":
        byte = np.frexp(amax)[1] - 1 + 127 - 7
    else:
        mant, ex = np.frexp(amax / 6.0)
        byte = np.where(mant > 0.5, ex, ex - 1) + 127
    byte = np.clip(np.where(amax > 0, byte, 1), 1, 254)
    scaled = (w * np.exp2(127.0 - byte)[:, None, :]).reshape(k, n).astype(np.float32)
    by_word = np.ascontiguousarray(scaled.reshape(k // 512, 128, 4, n).transpose(0, 1, 3, 2))
    if fmt == "e4m3":
        words = by_word.astype(ml_dtypes.float8_e4m3fn).view(np.uint8)
    else:
        c = by_word.astype(ml_dtypes.float4_e2m1fn).view(np.uint8) & 0xF
        words = (c[..., 0::2] | (c[..., 1::2] << 4)).reshape(k // 512, 128, 2 * n)
    return np.ascontiguousarray(words), np.ascontiguousarray(byte.astype(np.uint8).reshape(k // 512, 16, n))


def unpack_weight(words, scales, fmt):
    g, _, n = scales.shape
    words = np.ascontiguousarray(words).reshape(g, 128, n, -1)
    if fmt == "e4m3":
        vals = words.view(ml_dtypes.float8_e4m3fn).astype(np.float64)
    else:
        nib = np.empty((g, 128, n, 4), np.uint8)
        nib[..., 0::2] = words & 0xF
        nib[..., 1::2] = words >> 4
        vals = E2M1[nib]
    vals = vals * np.repeat(np.exp2(scales.astype(np.float64) - 127.0), 8, axis=1)[..., None]
    return vals.transpose(0, 1, 3, 2).reshape(g * 512, n)


def sigmoid(v):
    return 1.0 / (1.0 + np.exp(-v))


K, R, F, T, J = 512, 128, 512, 2048, 512


def setup_inputs():
    n = np.random.standard_normal
    idx = np.random.permutation(T)[:J]
    fk = mx_kscale(K)
    tabp = pack_weight(n((K, T)) / fk[:, None], "e4m3")
    dtabp = pack_weight(n((K, T)) / fk[:, None], "e4m3")
    return {
        "tab_words": tabp[0],
        "tab_scales": tabp[1],
        "dtab_words": dtabp[0],
        "dtab_scales": dtabp[1],
        "w1": (n((K, R)) * 1 / np.sqrt(K) * fk[:, None]).astype(np.float32),
        "gain": (np.random.uniform(0.5, 1.5, (R, 1))).astype(np.float32),
        "og": (np.random.uniform(0.5, 2.0, (R, 1))).astype(np.float32),
        "base": (0.3 * n((R, J))).astype(np.float32),
        "offs": striped(idx),
    }


def reference(tab_words, tab_scales, dtab_words, dtab_scales, w1, gain, og, base, offs):
    idx = unstriped(offs)
    tabu = unpack_weight(tab_words, tab_scales, "e4m3")
    dtabu = unpack_weight(dtab_words, dtab_scales, "e4m3")
    w1q = mxq(f64(w1), 0, "e4m3")
    tabidxg = tabu[:, idx]
    a = w1q.T @ tabidxg
    dtabidxg = dtabu[:, idx]
    ta = w1q.T @ dtabidxg
    n1 = np.sqrt(np.mean(np.square(a), axis=1, keepdims=True) + 0.01)
    s = a / n1 * f64(gain)
    tn1 = np.mean(ta * a * 2.0, axis=1, keepdims=True) * 0.5 / n1
    ts = (ta - tn1 * a / n1) / n1 * f64(gain)
    tu1 = ts * sigmoid(s) + ts * sigmoid(s) * (1.0 - sigmoid(s)) * s
    y = tu1 * f64(og) + f64(base)
    return y

@@ -1,0 +1,161 @@
+from contextlib import ExitStack
+
+import concourse.mybir as mybir
+
+F32 = mybir.dt.float32
+BF16 = mybir.dt.bfloat16
+I32 = mybir.dt.int32
+U32 = mybir.dt.uint32
+U16 = mybir.dt.uint16
+U8 = mybir.dt.uint8
+FP8X4 = mybir.dt.float8_e4m3fn_x4
+ALU = mybir.AluOpType
+ACT = mybir.ActivationFunctionType
+
+P = 128
+K, R, T, J = 512, 128, 2048, 512
+PACK = 4
+HALF = J // 2
+EPS = 0.01
+FLOPS = 2 * 2 * K * R * J
+DTAB_PLANE = 4
+
+
+def tile_attend_tcslotnorm_kernel(tc, tab_words, tab_scales, dtab_words, dtab_scales, w1, gain, og, base, offs, out):
+    nc = tc.nc
+    halves = [slice(h * HALF, (h + 1) * HALF) for h in range(2)]
+    with ExitStack() as ctx:
+        sb = ctx.enter_context(tc.tile_pool(name="sb", bufs=1))
+        ps = ctx.enter_context(tc.psum_pool(name="ps", bufs=1))
+
+        offsets = sb.tile([P, J // 16], U16, name="offsets")
+        nc.sync.dma_start(offsets[:], offs)
+
+        tab_plane = sb.tile([P, T], U8, name="tab_plane")
+        dtab_plane = sb.tile([P, T], U8, name="dtab_plane")
+        nc.vector.memset(tab_plane[:].bitcast(I32), 0)
+        ones = sb.tile([P, 1], F32, name="ones", tag="ones_then_tab")
+        nc.vector.memset(ones[:], 1.0)
+        eps = sb.tile([P, 1], F32, name="eps")
+        nc.vector.tensor_scalar(eps[:], ones[:], EPS, None, ALU.mult)
+        nc.vector.memset(dtab_plane[:].bitcast(I32), 0)
+
+        def load_plane(plane, scales, first, queues):
+            for q in range(4):
+                queues[q % len(queues)].dma_start(
+                    plane[32 * q + first : 32 * q + first + 4, :].bitcast(I32),
+                    scales[0, 4 * q : 4 * q + 4, :].bitcast(I32),
+                )
+
+        def load_words(words, name, tag):
+            pool_words = sb.tile([P, T], I32, name=name, tag=tag)
+            nc.sync.dma_start(pool_words[:], words[0].rearrange("p n t -> p (n t)").bitcast(I32))
+            return pool_words
+
+        w_raw = sb.tile([P, PACK, R], F32, name="w_raw", tag="w_then_dtab")
+        nc.sync.dma_start(w_raw[:], w1.rearrange("(p t) r -> p t r", t=PACK))
+        load_plane(tab_plane, tab_scales, 0, (nc.sync, nc.scalar))
+        tab_pool = load_words(tab_words, "tab_pool", "ones_then_tab")
+        load_plane(dtab_plane, dtab_scales, DTAB_PLANE, (nc.sync,))
+
+        gain_sb = sb.tile([P, 1], F32, name="gain_sb")
+        og_sb = sb.tile([P, 1], F32, name="og_sb")
+        nc.gpsimd.dma_start(gain_sb[:], gain)
+        nc.gpsimd.dma_start(og_sb[:], og)
+        minus_half = sb.tile([P, 1], F32, name="minus_half")
+        nc.gpsimd.memset(minus_half[:], -0.5)
+        warm = sb.tile([P, 1], F32, name="warm")
+        nc.scalar.activation(warm[:], eps[:], ACT.Silu)
+
+        w_bf = sb.tile([P, R, PACK], BF16, name="w_bf", tag="w_then_base", align_bytes=64)
+        nc.scalar.copy(w_bf[:], w_raw[:].rearrange("p t r -> p r t"))
+        w_codes = sb.tile([P, R], U32, name="w_codes", align_bytes=64)
+        w_scales = sb.tile([P, R], U8, name="w_scales", align_bytes=64)
+
+        def gather_plane(plane, name):
+            picked = sb.tile([P, J], U8, name=name, align_bytes=64)
+            nc.vector.tensor_copy(picked[:], plane[:].indirect(offsets[:]))
+            return picked
+
+        tab_picked = gather_plane(tab_plane, "tab_picked")
+        nc.vector.quantize_mx(
+            out=w_codes[:].bitcast(FP8X4), scales=w_scales[:], in_=w_bf[:].rearrange("p r t -> p (r t)")
+        )
+        dtab_pool = load_words(dtab_words, "dtab_pool", "w_then_dtab")
+        base_sb = sb.tile([P, J], F32, name="base_sb", tag="w_then_base", align_bytes=64)
+        nc.sync.dma_start(base_sb[:], base)
+
+        gains = sb.tile([P, 3], F32, name="gains")
+        nc.gpsimd.tensor_copy(gains[:, 0:1], gain_sb[:])
+        nc.gpsimd.tensor_scalar(gains[:, 1:2], gain_sb[:], 0.5, None, ALU.mult)
+        nc.gpsimd.tensor_scalar(gains[:, 2:3], gain_sb[:], og_sb[:], -0.5, ALU.mult, ALU.mult)
+
+        def product(pool_words, picked_scales, first, name):
+            banks = []
+            for h in range(2):
+                picked = sb.tile([P, HALF], U32, name="%s_words%d" % (name, h), align_bytes=64)
+                lst = offsets[:, h * (HALF // 16) : (h + 1) * (HALF // 16)]
+                nc.vector.tensor_copy(picked[:], pool_words[:].bitcast(U32).indirect(lst))
+                bank = ps.tile([P, HALF], F32, name="%s_bank%d" % (name, h))
+                nc.tensor.matmul_mx(
+                    out=bank[:],
+                    lhsT=w_codes[:].bitcast(FP8X4),
+                    lhsT_scale=w_scales[:],
+                    rhs=picked[:].bitcast(FP8X4),
+                    rhs_scale=picked_scales[first:P, halves[h]],
+                    start=True,
+                    stop=True,
+                )
+                banks.append(bank)
+            return banks
+
+        a_ps = product(tab_pool, tab_picked, 0, "a")
+        dtab_picked = gather_plane(dtab_plane, "dtab_picked")
+        ta_ps = product(dtab_pool, dtab_picked, DTAB_PLANE, "ta")
+
+        def half_tiles(name):
+            return [sb.tile([P, HALF], F32, name="%s%d" % (name, h)) for h in range(2)]
+
+        def column(name):
+            return sb.tile([P, 1], F32, name=name)
+
+        squares, a_sb = half_tiles("squares"), half_tiles("a_sb")
+        ssq = [column("ssq0"), column("ssq1")]
+        part, msq, rinv = column("part"), column("msq"), column("rinv")
+        nc.scalar.activation(squares[0][:], a_ps[0][:], ACT.Square, accum_out=ssq[0][:])
+        nc.scalar.activation(part[:], ssq[0][:], ACT.Identity, bias=eps[:], scale=1.0 / J)
+        nc.scalar.copy(a_sb[0][:], a_ps[0][:])
+        nc.scalar.activation(squares[1][:], a_ps[1][:], ACT.Square, accum_out=ssq[1][:])
+        nc.scalar.activation(msq[:], ssq[1][:], ACT.Identity, bias=part[:], scale=1.0 / J)
+        nc.scalar.copy(a_sb[1][:], a_ps[1][:])
+        nc.gpsimd.tensor_tensor(rinv[:], msq[:], minus_half[:], ALU.pow)
+        factors = sb.tile([P, 3], F32, name="factors")
+        nc.scalar.activation(factors[:], gains[:], ACT.Identity, scale=rinv[:])
+        pull = column("pull")
+        nc.gpsimd.tensor_scalar(pull[:], rinv[:], rinv[:], -1.0 / J, ALU.mult, ALU.mult)
+
+        silu, silu_m1, tanh = half_tiles("silu"), half_tiles("silu_m1"), half_tiles("tanh")
+        for h in range(2):
+            nc.scalar.activation(silu[h][:], a_sb[h][:], ACT.Silu, scale=factors[:, 0:1])
+            nc.scalar.activation(tanh[h][:], a_sb[h][:], ACT.Tanh, scale=factors[:, 1:2])
+            nc.scalar.activation(silu_m1[h][:], silu[h][:], ACT.Identity, bias=-1.0)
+
+        gate, proj, gated, res = (half_tiles(n) for n in ("gate", "proj", "gated", "res"))
+        dot = [column("dot0"), column("dot1")]
+        coef = column("coef")
+        for h in range(2):
+            nc.vector.scalar_tensor_tensor(
+                gate[h][:], ta_ps[h][:], 1.0, a_sb[h][:], ALU.mult, ALU.mult, accum_out=dot[h][:]
+            )
+        nc.vector.scalar_tensor_tensor(gate[0][:], tanh[0][:], 1.0, silu_m1[0][:], ALU.subtract, ALU.mult)
+        nc.vector.tensor_scalar(coef[:], dot[0][:], dot[1][:], pull[:], ALU.add, ALU.mult)
+        nc.vector.scalar_tensor_tensor(gate[1][:], tanh[1][:], 1.0, silu_m1[1][:], ALU.subtract, ALU.mult)
+        for h in range(2):
+            nc.vector.scalar_tensor_tensor(proj[h][:], a_sb[h][:], coef[:], ta_ps[h][:], ALU.mult, ALU.add)
+        for h in range(2):
+            nc.vector.scalar_tensor_tensor(gated[h][:], gate[h][:], 2.0, proj[h][:], ALU.subtract, ALU.mult)
+        for h in range(2):
+            nc.vector.scalar_tensor_tensor(
+                res[h][:], gated[h][:], factors[:, 2:3], base_sb[:, halves[h]], ALU.mult, ALU.add
+            )
+            nc.sync.dma_start(out[:, halves[h]], res[h][:])

@@ -54,26 +54,22 @@ def tile_attend_tcslotnorm_kernel(tc, tab_words, tab_scales, dtab_words, dtab_sc
 
         w_raw = sb.tile([P, PACK, R], F32, name="w_raw", tag="w_then_dtab")
         nc.sync.dma_start(w_raw[:], w1.rearrange("(p t) r -> p t r", t=PACK))
-        load_plane(tab_plane, tab_scales, 0, (nc.sync, nc.scalar))
+        load_plane(tab_plane, tab_scales, 0, (nc.sync,))
         tab_pool = load_words(tab_words, "tab_pool", "ones_then_tab")
         load_plane(dtab_plane, dtab_scales, DTAB_PLANE, (nc.sync,))
 
-        gain_sb = sb.tile([P, 1], F32, name="gain_sb")
-        og_sb = sb.tile([P, 1], F32, name="og_sb")
-        nc.gpsimd.dma_start(gain_sb[:], gain)
-        nc.gpsimd.dma_start(og_sb[:], og)
         minus_half = sb.tile([P, 1], F32, name="minus_half")
         nc.gpsimd.memset(minus_half[:], -0.5)
         warm = sb.tile([P, 1], F32, name="warm")
         nc.scalar.activation(warm[:], eps[:], ACT.Silu)
 
-        w_bf = sb.tile([P, R, PACK], BF16, name="w_bf", tag="w_then_base", align_bytes=64)
+        w_bf = sb.tile([P, R, PACK], BF16, name="w_bf", tag="w_then_gain", align_bytes=64)
         nc.scalar.copy(w_bf[:], w_raw[:].rearrange("p t r -> p r t"))
         w_codes = sb.tile([P, R], U32, name="w_codes", align_bytes=64)
         w_scales = sb.tile([P, R], U8, name="w_scales", align_bytes=64)
 
         def gather_plane(plane, name):
-            picked = sb.tile([P, J], U8, name=name, align_bytes=64)
+            picked = sb.tile([P, J], U8, name=name, tag=name, align_bytes=64)
             nc.vector.tensor_copy(picked[:], plane[:].indirect(offsets[:]))
             return picked
 
@@ -82,13 +78,8 @@ def tile_attend_tcslotnorm_kernel(tc, tab_words, tab_scales, dtab_words, dtab_sc
             out=w_codes[:].bitcast(FP8X4), scales=w_scales[:], in_=w_bf[:].rearrange("p r t -> p (r t)")
         )
         dtab_pool = load_words(dtab_words, "dtab_pool", "w_then_dtab")
-        base_sb = sb.tile([P, J], F32, name="base_sb", tag="w_then_base", align_bytes=64)
-        nc.sync.dma_start(base_sb[:], base)
-
-        gains = sb.tile([P, 3], F32, name="gains")
-        nc.gpsimd.tensor_copy(gains[:, 0:1], gain_sb[:])
-        nc.gpsimd.tensor_scalar(gains[:, 1:2], gain_sb[:], 0.5, None, ALU.mult)
-        nc.gpsimd.tensor_scalar(gains[:, 2:3], gain_sb[:], og_sb[:], -0.5, ALU.mult, ALU.mult)
+        gain_sb = sb.tile([P, 1], F32, name="gain_sb", tag="w_then_gain", align_bytes=64)
+        nc.sync.dma_start(gain_sb[:], gain)
 
         def product(pool_words, picked_scales, first, name):
             banks = []
@@ -110,52 +101,63 @@ def tile_attend_tcslotnorm_kernel(tc, tab_words, tab_scales, dtab_words, dtab_sc
             return banks
 
         a_ps = product(tab_pool, tab_picked, 0, "a")
+        base_sb = sb.tile([P, J], F32, name="base_sb", tag="ones_then_tab")
+        nc.sync.dma_start(base_sb[:], base)
+        og_sb = sb.tile([P, 1], F32, name="og_sb", tag="tab_picked", align_bytes=64)
+        nc.sync.dma_start(og_sb[:], og)
         dtab_picked = gather_plane(dtab_plane, "dtab_picked")
         ta_ps = product(dtab_pool, dtab_picked, DTAB_PLANE, "ta")
 
         def half_tiles(name):
-            return [sb.tile([P, HALF], F32, name="%s%d" % (name, h)) for h in range(2)]
+            return [sb.tile([P, HALF], F32, name="%s%d" % (name, h), tag="%s%d" % (name, h)) for h in range(2)]
 
         def column(name):
             return sb.tile([P, 1], F32, name=name)
 
-        squares, a_sb = half_tiles("squares"), half_tiles("a_sb")
-        ssq = [column("ssq0"), column("ssq1")]
-        part, msq, rinv = column("part"), column("msq"), column("rinv")
+        squares = half_tiles("squares")
+        ssq = [column("ssq0"), sb.tile([P, 1], F32, name="ssq1", tag="a_sb1")]
+        part = sb.tile([P, 1], F32, name="part", tag="a_sb0")
+        msq, rinv = column("msq"), column("rinv")
         nc.scalar.activation(squares[0][:], a_ps[0][:], ACT.Square, accum_out=ssq[0][:])
         nc.scalar.activation(part[:], ssq[0][:], ACT.Identity, bias=eps[:], scale=1.0 / J)
-        nc.scalar.copy(a_sb[0][:], a_ps[0][:])
         nc.scalar.activation(squares[1][:], a_ps[1][:], ACT.Square, accum_out=ssq[1][:])
         nc.scalar.activation(msq[:], ssq[1][:], ACT.Identity, bias=part[:], scale=1.0 / J)
-        nc.scalar.copy(a_sb[1][:], a_ps[1][:])
-        nc.gpsimd.tensor_tensor(rinv[:], msq[:], minus_half[:], ALU.pow)
-        factors = sb.tile([P, 3], F32, name="factors")
-        nc.scalar.activation(factors[:], gains[:], ACT.Identity, scale=rinv[:])
-        pull = column("pull")
-        nc.gpsimd.tensor_scalar(pull[:], rinv[:], rinv[:], -1.0 / J, ALU.mult, ALU.mult)
-
-        silu, silu_m1, tanh = half_tiles("silu"), half_tiles("silu_m1"), half_tiles("tanh")
+        a_sb = half_tiles("a_sb")
         for h in range(2):
-            nc.scalar.activation(silu[h][:], a_sb[h][:], ACT.Silu, scale=factors[:, 0:1])
-            nc.scalar.activation(tanh[h][:], a_sb[h][:], ACT.Tanh, scale=factors[:, 1:2])
-            nc.scalar.activation(silu_m1[h][:], silu[h][:], ACT.Identity, bias=-1.0)
+            nc.scalar.copy(a_sb[h][:], a_ps[h][:])
+        nc.gpsimd.tensor_tensor(rinv[:], msq[:], minus_half[:], ALU.pow)
+        rinv_sq = sb.tile([P, 1], F32, name="rinv_sq", tag="w_then_dtab")
+        nc.vector.reciprocal(rinv_sq[:], msq[:])
 
-        gate, proj, gated, res = (half_tiles(n) for n in ("gate", "proj", "gated", "res"))
+        s_scale, t_scale, out_scale = column("s_scale"), column("t_scale"), column("out_scale")
+        silu, silu_m1, tanh = half_tiles("silu"), half_tiles("silu_m1"), half_tiles("tanh")
+        nc.scalar.activation(s_scale[:], gain_sb[:], ACT.Identity, scale=rinv[:])
+        nc.scalar.activation(silu[0][:], a_ps[0][:], ACT.Silu, scale=s_scale[:])
+        nc.scalar.activation(t_scale[:], s_scale[:], ACT.Identity, scale=0.5)
+        nc.scalar.activation(silu_m1[0][:], silu[0][:], ACT.Identity, bias=-1.0)
+        nc.scalar.activation(tanh[0][:], a_ps[0][:], ACT.Tanh, scale=t_scale[:])
+        nc.scalar.activation(silu[1][:], a_ps[1][:], ACT.Silu, scale=s_scale[:])
+        nc.scalar.activation(tanh[1][:], a_ps[1][:], ACT.Tanh, scale=t_scale[:])
+        nc.scalar.activation(silu_m1[1][:], silu[1][:], ACT.Identity, bias=-1.0)
+        nc.scalar.activation(out_scale[:], og_sb[:], ACT.Identity, scale=t_scale[:])
+
+        cross, proj, gated, res = (half_tiles(n) for n in ("cross", "proj", "gated", "res"))
         dot = [column("dot0"), column("dot1")]
         coef = column("coef")
         for h in range(2):
             nc.vector.scalar_tensor_tensor(
-                gate[h][:], ta_ps[h][:], 1.0, a_sb[h][:], ALU.mult, ALU.mult, accum_out=dot[h][:]
+                cross[h][:], ta_ps[h][:], 1.0 / J, a_sb[h][:], ALU.mult, ALU.mult, accum_out=dot[h][:]
             )
-        nc.vector.scalar_tensor_tensor(gate[0][:], tanh[0][:], 1.0, silu_m1[0][:], ALU.subtract, ALU.mult)
-        nc.vector.tensor_scalar(coef[:], dot[0][:], dot[1][:], pull[:], ALU.add, ALU.mult)
-        nc.vector.scalar_tensor_tensor(gate[1][:], tanh[1][:], 1.0, silu_m1[1][:], ALU.subtract, ALU.mult)
+        nc.vector.tensor_scalar(coef[:], dot[0][:], dot[1][:], rinv_sq[:], ALU.add, ALU.mult)
         for h in range(2):
-            nc.vector.scalar_tensor_tensor(proj[h][:], a_sb[h][:], coef[:], ta_ps[h][:], ALU.mult, ALU.add)
+            nc.vector.scalar_tensor_tensor(proj[h][:], a_sb[h][:], coef[:], ta_ps[h][:], ALU.mult, ALU.subtract)
+        gate = half_tiles("a_sb")
+        for h in range(2):
+            nc.vector.scalar_tensor_tensor(gate[h][:], tanh[h][:], 1.0, silu_m1[h][:], ALU.subtract, ALU.mult)
         for h in range(2):
             nc.vector.scalar_tensor_tensor(gated[h][:], gate[h][:], 2.0, proj[h][:], ALU.subtract, ALU.mult)
         for h in range(2):
             nc.vector.scalar_tensor_tensor(
-                res[h][:], gated[h][:], factors[:, 2:3], base_sb[:, halves[h]], ALU.mult, ALU.add
+                res[h][:], gated[h][:], out_scale[:], base_sb[:, halves[h]], ALU.mult, ALU.add
             )
             nc.sync.dma_start(out[:, halves[h]], res[h][:])

@@ -15,10 +15,13 @@ ACT = mybir.ActivationFunctionType
 P = 128
 K, R, T, J = 512, 128, 2048, 512
 PACK = 4
+BLOCKS = K // 32
+QUADRANT = 32
+LIST_ROWS = 16
 HALF = J // 2
 EPS = 0.01
+TAB_FIRST, DTAB_FIRST = 0, 4
 FLOPS = 2 * 2 * K * R * J
-DTAB_PLANE = 4
 
 
 def tile_attend_tcslotnorm_kernel(tc, tab_words, tab_scales, dtab_words, dtab_scales, w1, gain, og, base, offs, out):
@@ -28,85 +31,42 @@ def tile_attend_tcslotnorm_kernel(tc, tab_words, tab_scales, dtab_words, dtab_sc
         sb = ctx.enter_context(tc.tile_pool(name="sb", bufs=1))
         ps = ctx.enter_context(tc.psum_pool(name="ps", bufs=1))
 
-        offsets = sb.tile([P, J // 16], U16, name="offsets")
-        nc.sync.dma_start(offsets[:], offs)
-
-        tab_plane = sb.tile([P, T], U8, name="tab_plane")
-        dtab_plane = sb.tile([P, T], U8, name="dtab_plane")
-        nc.vector.memset(tab_plane[:].bitcast(I32), 0)
-        ones = sb.tile([P, 1], F32, name="ones", tag="ones_then_tab")
-        nc.vector.memset(ones[:], 1.0)
-        eps = sb.tile([P, 1], F32, name="eps")
-        nc.vector.tensor_scalar(eps[:], ones[:], EPS, None, ALU.mult)
-        nc.vector.memset(dtab_plane[:].bitcast(I32), 0)
-
-        def load_plane(plane, scales, first, queues):
-            for q in range(4):
-                queues[q % len(queues)].dma_start(
-                    plane[32 * q + first : 32 * q + first + 4, :].bitcast(I32),
-                    scales[0, 4 * q : 4 * q + 4, :].bitcast(I32),
+        def load_plane(plane, scales, first):
+            rows = BLOCKS * QUADRANT // P
+            for f in range(rows):
+                nc.sync.dma_start(
+                    plane[first + f : P : QUADRANT, :].bitcast(I32),
+                    scales[0, f:BLOCKS:rows, :].bitcast(I32),
                 )
 
         def load_words(words, name, tag):
-            pool_words = sb.tile([P, T], I32, name=name, tag=tag)
-            nc.sync.dma_start(pool_words[:], words[0].rearrange("p n t -> p (n t)").bitcast(I32))
-            return pool_words
-
-        w_raw = sb.tile([P, PACK, R], F32, name="w_raw", tag="w_then_dtab")
-        nc.sync.dma_start(w_raw[:], w1.rearrange("(p t) r -> p t r", t=PACK))
-        load_plane(tab_plane, tab_scales, 0, (nc.sync,))
-        tab_pool = load_words(tab_words, "tab_pool", "ones_then_tab")
-        load_plane(dtab_plane, dtab_scales, DTAB_PLANE, (nc.sync,))
-
-        minus_half = sb.tile([P, 1], F32, name="minus_half")
-        nc.gpsimd.memset(minus_half[:], -0.5)
-        warm = sb.tile([P, 1], F32, name="warm")
-        nc.scalar.activation(warm[:], eps[:], ACT.Silu)
-
-        w_bf = sb.tile([P, R, PACK], BF16, name="w_bf", tag="w_then_gain", align_bytes=64)
-        nc.scalar.copy(w_bf[:], w_raw[:].rearrange("p t r -> p r t"))
-        w_codes = sb.tile([P, R], U32, name="w_codes", align_bytes=64)
-        w_scales = sb.tile([P, R], U8, name="w_scales", align_bytes=64)
+            table = sb.tile([P, T], I32, name=name, tag=tag)
+            nc.sync.dma_start(table[:], words[0].rearrange("p n t -> p (n t)").bitcast(I32))
+            return table
 
         def gather_plane(plane, name):
-            picked = sb.tile([P, J], U8, name=name, tag=name, align_bytes=64)
-            nc.vector.tensor_copy(picked[:], plane[:].indirect(offsets[:]))
-            return picked
+            picked_plane = sb.tile([P, J], U8, name=name, align_bytes=64)
+            nc.vector.tensor_copy(picked_plane[:], plane[:].indirect(offsets[:]))
+            return picked_plane
 
-        tab_picked = gather_plane(tab_plane, "tab_picked")
-        nc.vector.quantize_mx(
-            out=w_codes[:].bitcast(FP8X4), scales=w_scales[:], in_=w_bf[:].rearrange("p r t -> p (r t)")
-        )
-        dtab_pool = load_words(dtab_words, "dtab_pool", "w_then_dtab")
-        gain_sb = sb.tile([P, 1], F32, name="gain_sb", tag="w_then_gain", align_bytes=64)
-        nc.sync.dma_start(gain_sb[:], gain)
-
-        def product(pool_words, picked_scales, first, name):
+        def product(table, picked_plane, first, name):
             banks = []
             for h in range(2):
-                picked = sb.tile([P, HALF], U32, name="%s_words%d" % (name, h), align_bytes=64)
-                lst = offsets[:, h * (HALF // 16) : (h + 1) * (HALF // 16)]
-                nc.vector.tensor_copy(picked[:], pool_words[:].bitcast(U32).indirect(lst))
+                picked_words = sb.tile([P, HALF], U32, name="%s_words%d" % (name, h), align_bytes=64)
+                half_list = offsets[:, h * (HALF // LIST_ROWS) : (h + 1) * (HALF // LIST_ROWS)]
+                nc.vector.tensor_copy(picked_words[:], table[:].bitcast(U32).indirect(half_list))
                 bank = ps.tile([P, HALF], F32, name="%s_bank%d" % (name, h))
                 nc.tensor.matmul_mx(
                     out=bank[:],
                     lhsT=w_codes[:].bitcast(FP8X4),
-                    lhsT_scale=w_scales[:],
-                    rhs=picked[:].bitcast(FP8X4),
-                    rhs_scale=picked_scales[first:P, halves[h]],
+                    lhsT_scale=w_plane[:],
+                    rhs=picked_words[:].bitcast(FP8X4),
+                    rhs_scale=picked_plane[first:P, halves[h]],
                     start=True,
                     stop=True,
                 )
                 banks.append(bank)
             return banks
-
-        a_ps = product(tab_pool, tab_picked, 0, "a")
-        base_sb = sb.tile([P, J], F32, name="base_sb", tag="ones_then_tab")
-        nc.sync.dma_start(base_sb[:], base)
-        og_sb = sb.tile([P, 1], F32, name="og_sb", tag="tab_picked", align_bytes=64)
-        nc.sync.dma_start(og_sb[:], og)
-        dtab_picked = gather_plane(dtab_plane, "dtab_picked")
-        ta_ps = product(dtab_pool, dtab_picked, DTAB_PLANE, "ta")
 
         def half_tiles(name):
             return [sb.tile([P, HALF], F32, name="%s%d" % (name, h), tag="%s%d" % (name, h)) for h in range(2)]
@@ -114,34 +74,79 @@ def tile_attend_tcslotnorm_kernel(tc, tab_words, tab_scales, dtab_words, dtab_sc
         def column(name):
             return sb.tile([P, 1], F32, name=name)
 
+        offsets = sb.tile([P, J // LIST_ROWS], U16, name="offsets")
+        nc.sync.dma_start(offsets[:], offs)
+
+        tab_plane = sb.tile([P, T], U8, name="tab_plane", tag="tab_plane_then_og")
+        dtab_plane = sb.tile([P, T], U8, name="dtab_plane")
+        nc.vector.memset(tab_plane[:].bitcast(I32), 0)
+        ones = sb.tile([P, 1], F32, name="ones", tag="ones_then_tab_then_base")
+        nc.vector.memset(ones[:], 1.0)
+        eps = column("eps")
+        nc.vector.tensor_scalar(eps[:], ones[:], EPS, None, ALU.mult)
+        nc.vector.memset(dtab_plane[:].bitcast(I32), 0)
+
+        w_raw = sb.tile([P, PACK, R], F32, name="w_raw")
+        nc.sync.dma_start(w_raw[:], w1.rearrange("(p t) r -> p t r", t=PACK))
+        load_plane(tab_plane, tab_scales, TAB_FIRST)
+        tab = load_words(tab_words, "tab", "ones_then_tab_then_base")
+        load_plane(dtab_plane, dtab_scales, DTAB_FIRST)
+
+        minus_half = column("minus_half")
+        nc.gpsimd.memset(minus_half[:], -0.5)
+        warm = sb.tile([P, 1], F32, name="warm", tag="warm_then_dtab_then_rinv_sq")
+        nc.scalar.activation(warm[:], eps[:], ACT.Silu)
+
+        w_bf = sb.tile([P, R, PACK], BF16, name="w_bf", tag="w_bf_then_gain", align_bytes=64)
+        nc.scalar.copy(w_bf[:], w_raw[:].rearrange("p t r -> p r t"))
+        w_codes = sb.tile([P, R], U32, name="w_codes", align_bytes=64)
+        w_plane = sb.tile([P, R], U8, name="w_plane", align_bytes=64)
+
+        tab_picked = gather_plane(tab_plane, "tab_picked")
+        nc.vector.quantize_mx(
+            out=w_codes[:].bitcast(FP8X4), scales=w_plane[:], in_=w_bf[:].rearrange("p r t -> p (r t)")
+        )
+
+        dtab = load_words(dtab_words, "dtab", "warm_then_dtab_then_rinv_sq")
+        gain_sb = sb.tile([P, 1], F32, name="gain_sb", tag="w_bf_then_gain", align_bytes=64)
+        nc.sync.dma_start(gain_sb[:], gain)
+        og_sb = sb.tile([P, 1], F32, name="og_sb", tag="tab_plane_then_og")
+        nc.sync.dma_start(og_sb[:], og)
+
+        a_ps = product(tab, tab_picked, TAB_FIRST, "a")
+        base_sb = sb.tile([P, J], F32, name="base_sb", tag="ones_then_tab_then_base")
+        nc.sync.dma_start(base_sb[:], base)
+        dtab_picked = gather_plane(dtab_plane, "dtab_picked")
+        ta_ps = product(dtab, dtab_picked, DTAB_FIRST, "ta")
+
         squares = half_tiles("squares")
         ssq = [column("ssq0"), sb.tile([P, 1], F32, name="ssq1", tag="a_sb1")]
-        part = sb.tile([P, 1], F32, name="part", tag="a_sb0")
+        msq_first = sb.tile([P, 1], F32, name="msq_first", tag="a_sb0")
         msq, rinv = column("msq"), column("rinv")
         nc.scalar.activation(squares[0][:], a_ps[0][:], ACT.Square, accum_out=ssq[0][:])
-        nc.scalar.activation(part[:], ssq[0][:], ACT.Identity, bias=eps[:], scale=1.0 / J)
+        nc.scalar.activation(msq_first[:], ssq[0][:], ACT.Identity, bias=eps[:], scale=1.0 / J)
         nc.scalar.activation(squares[1][:], a_ps[1][:], ACT.Square, accum_out=ssq[1][:])
-        nc.scalar.activation(msq[:], ssq[1][:], ACT.Identity, bias=part[:], scale=1.0 / J)
+        nc.scalar.activation(msq[:], ssq[1][:], ACT.Identity, bias=msq_first[:], scale=1.0 / J)
         a_sb = half_tiles("a_sb")
         for h in range(2):
             nc.scalar.copy(a_sb[h][:], a_ps[h][:])
         nc.gpsimd.tensor_tensor(rinv[:], msq[:], minus_half[:], ALU.pow)
-        rinv_sq = sb.tile([P, 1], F32, name="rinv_sq", tag="w_then_dtab")
+        rinv_sq = sb.tile([P, 1], F32, name="rinv_sq", tag="warm_then_dtab_then_rinv_sq")
         nc.vector.reciprocal(rinv_sq[:], msq[:])
 
-        s_scale, t_scale, out_scale = column("s_scale"), column("t_scale"), column("out_scale")
+        s_scale, half_scale, out_scale = column("s_scale"), column("half_scale"), column("out_scale")
         silu, silu_m1, tanh = half_tiles("silu"), half_tiles("silu_m1"), half_tiles("tanh")
         nc.scalar.activation(s_scale[:], gain_sb[:], ACT.Identity, scale=rinv[:])
         nc.scalar.activation(silu[0][:], a_ps[0][:], ACT.Silu, scale=s_scale[:])
-        nc.scalar.activation(t_scale[:], s_scale[:], ACT.Identity, scale=0.5)
+        nc.scalar.activation(half_scale[:], s_scale[:], ACT.Identity, scale=0.5)
         nc.scalar.activation(silu_m1[0][:], silu[0][:], ACT.Identity, bias=-1.0)
-        nc.scalar.activation(tanh[0][:], a_ps[0][:], ACT.Tanh, scale=t_scale[:])
+        nc.scalar.activation(tanh[0][:], a_ps[0][:], ACT.Tanh, scale=half_scale[:])
         nc.scalar.activation(silu[1][:], a_ps[1][:], ACT.Silu, scale=s_scale[:])
-        nc.scalar.activation(tanh[1][:], a_ps[1][:], ACT.Tanh, scale=t_scale[:])
+        nc.scalar.activation(tanh[1][:], a_ps[1][:], ACT.Tanh, scale=half_scale[:])
         nc.scalar.activation(silu_m1[1][:], silu[1][:], ACT.Identity, bias=-1.0)
-        nc.scalar.activation(out_scale[:], og_sb[:], ACT.Identity, scale=t_scale[:])
+        nc.gpsimd.tensor_tensor(out_scale[:], og_sb[:], half_scale[:], ALU.mult)
 
-        cross, proj, gated, res = (half_tiles(n) for n in ("cross", "proj", "gated", "res"))
+        cross, proj, gated, result = (half_tiles(name) for name in ("cross", "proj", "gated", "result"))
         dot = [column("dot0"), column("dot1")]
         coef = column("coef")
         for h in range(2):
@@ -149,15 +154,16 @@ def tile_attend_tcslotnorm_kernel(tc, tab_words, tab_scales, dtab_words, dtab_sc
                 cross[h][:], ta_ps[h][:], 1.0 / J, a_sb[h][:], ALU.mult, ALU.mult, accum_out=dot[h][:]
             )
         nc.vector.tensor_scalar(coef[:], dot[0][:], dot[1][:], rinv_sq[:], ALU.add, ALU.mult)
+        gate = [sb.tile([P, HALF], F32, name="gate0", tag="cross1")]
+        nc.vector.scalar_tensor_tensor(gate[0][:], tanh[0][:], 1.0, silu_m1[0][:], ALU.subtract, ALU.mult)
         for h in range(2):
             nc.vector.scalar_tensor_tensor(proj[h][:], a_sb[h][:], coef[:], ta_ps[h][:], ALU.mult, ALU.subtract)
-        gate = half_tiles("a_sb")
-        for h in range(2):
-            nc.vector.scalar_tensor_tensor(gate[h][:], tanh[h][:], 1.0, silu_m1[h][:], ALU.subtract, ALU.mult)
+        gate.append(sb.tile([P, HALF], F32, name="gate1", tag="a_sb0"))
+        nc.vector.scalar_tensor_tensor(gate[1][:], tanh[1][:], 1.0, silu_m1[1][:], ALU.subtract, ALU.mult)
         for h in range(2):
             nc.vector.scalar_tensor_tensor(gated[h][:], gate[h][:], 2.0, proj[h][:], ALU.subtract, ALU.mult)
         for h in range(2):
             nc.vector.scalar_tensor_tensor(
-                res[h][:], gated[h][:], out_scale[:], base_sb[:, halves[h]], ALU.mult, ALU.add
+                result[h][:], gated[h][:], out_scale[:], base_sb[:, halves[h]], ALU.mult, ALU.add
             )
-            nc.sync.dma_start(out[:, halves[h]], res[h][:])
+            nc.sync.dma_start(out[:, halves[h]], result[h][:])

from contextlib import ExitStack

import concourse.mybir as mybir

F32 = mybir.dt.float32
BF16 = mybir.dt.bfloat16
I32 = mybir.dt.int32
U32 = mybir.dt.uint32
U16 = mybir.dt.uint16
U8 = mybir.dt.uint8
FP8X4 = mybir.dt.float8_e4m3fn_x4
ALU = mybir.AluOpType
ACT = mybir.ActivationFunctionType

P = 128
K, R, T, J = 512, 128, 2048, 512
PACK = 4
BLOCKS = K // 32
QUADRANT = 32
LIST_ROWS = 16
HALF = J // 2
EPS = 0.01
TAB_FIRST, DTAB_FIRST = 0, 4
FLOPS = 2 * 2 * K * R * J


def tile_attend_tcslotnorm_kernel(tc, tab_words, tab_scales, dtab_words, dtab_scales, w1, gain, og, base, offs, out):
    nc = tc.nc
    halves = [slice(h * HALF, (h + 1) * HALF) for h in range(2)]
    with ExitStack() as ctx:
        sb = ctx.enter_context(tc.tile_pool(name="sb", bufs=1))
        ps = ctx.enter_context(tc.psum_pool(name="ps", bufs=1))

        def load_plane(plane, scales, first):
            rows = BLOCKS * QUADRANT // P
            for f in range(rows):
                nc.sync.dma_start(
                    plane[first + f : P : QUADRANT, :].bitcast(I32),
                    scales[0, f:BLOCKS:rows, :].bitcast(I32),
                )

        def load_words(words, name, tag):
            table = sb.tile([P, T], I32, name=name, tag=tag)
            nc.sync.dma_start(table[:], words[0].rearrange("p n t -> p (n t)").bitcast(I32))
            return table

        def gather_plane(plane, name):
            picked_plane = sb.tile([P, J], U8, name=name, align_bytes=64)
            nc.vector.tensor_copy(picked_plane[:], plane[:].indirect(offsets[:]))
            return picked_plane

        def product(table, picked_plane, first, name):
            banks = []
            for h in range(2):
                picked_words = sb.tile([P, HALF], U32, name="%s_words%d" % (name, h), align_bytes=64)
                half_list = offsets[:, h * (HALF // LIST_ROWS) : (h + 1) * (HALF // LIST_ROWS)]
                nc.vector.tensor_copy(picked_words[:], table[:].bitcast(U32).indirect(half_list))
                bank = ps.tile([P, HALF], F32, name="%s_bank%d" % (name, h))
                nc.tensor.matmul_mx(
                    out=bank[:],
                    lhsT=w_codes[:].bitcast(FP8X4),
                    lhsT_scale=w_plane[:],
                    rhs=picked_words[:].bitcast(FP8X4),
                    rhs_scale=picked_plane[first:P, halves[h]],
                    start=True,
                    stop=True,
                )
                banks.append(bank)
            return banks

        def half_tiles(name):
            return [sb.tile([P, HALF], F32, name="%s%d" % (name, h), tag="%s%d" % (name, h)) for h in range(2)]

        def column(name):
            return sb.tile([P, 1], F32, name=name)

        offsets = sb.tile([P, J // LIST_ROWS], U16, name="offsets")
        nc.sync.dma_start(offsets[:], offs)

        tab_plane = sb.tile([P, T], U8, name="tab_plane", tag="tab_plane_then_og")
        dtab_plane = sb.tile([P, T], U8, name="dtab_plane")
        nc.vector.memset(tab_plane[:].bitcast(I32), 0)
        ones = sb.tile([P, 1], F32, name="ones", tag="ones_then_tab_then_base")
        nc.vector.memset(ones[:], 1.0)
        eps = column("eps")
        nc.vector.tensor_scalar(eps[:], ones[:], EPS, None, ALU.mult)
        nc.vector.memset(dtab_plane[:].bitcast(I32), 0)

        w_raw = sb.tile([P, PACK, R], F32, name="w_raw")
        nc.sync.dma_start(w_raw[:], w1.rearrange("(p t) r -> p t r", t=PACK))
        load_plane(tab_plane, tab_scales, TAB_FIRST)
        tab = load_words(tab_words, "tab", "ones_then_tab_then_base")
        load_plane(dtab_plane, dtab_scales, DTAB_FIRST)

        minus_half = column("minus_half")
        nc.gpsimd.memset(minus_half[:], -0.5)
        warm = sb.tile([P, 1], F32, name="warm", tag="warm_then_dtab_then_rinv_sq")
        nc.scalar.activation(warm[:], eps[:], ACT.Silu)

        w_bf = sb.tile([P, R, PACK], BF16, name="w_bf", tag="w_bf_then_gain", align_bytes=64)
        nc.scalar.copy(w_bf[:], w_raw[:].rearrange("p t r -> p r t"))
        w_codes = sb.tile([P, R], U32, name="w_codes", align_bytes=64)
        w_plane = sb.tile([P, R], U8, name="w_plane", align_bytes=64)

        tab_picked = gather_plane(tab_plane, "tab_picked")
        nc.vector.quantize_mx(
            out=w_codes[:].bitcast(FP8X4), scales=w_plane[:], in_=w_bf[:].rearrange("p r t -> p (r t)")
        )

        dtab = load_words(dtab_words, "dtab", "warm_then_dtab_then_rinv_sq")
        gain_sb = sb.tile([P, 1], F32, name="gain_sb", tag="w_bf_then_gain", align_bytes=64)
        nc.sync.dma_start(gain_sb[:], gain)
        og_sb = sb.tile([P, 1], F32, name="og_sb", tag="tab_plane_then_og")
        nc.sync.dma_start(og_sb[:], og)

        a_ps = product(tab, tab_picked, TAB_FIRST, "a")
        base_sb = sb.tile([P, J], F32, name="base_sb", tag="ones_then_tab_then_base")
        nc.sync.dma_start(base_sb[:], base)
        dtab_picked = gather_plane(dtab_plane, "dtab_picked")
        ta_ps = product(dtab, dtab_picked, DTAB_FIRST, "ta")

        squares = half_tiles("squares")
        ssq = [column("ssq0"), sb.tile([P, 1], F32, name="ssq1", tag="a_sb1")]
        msq_first = sb.tile([P, 1], F32, name="msq_first", tag="a_sb0")
        msq, rinv = column("msq"), column("rinv")
        nc.scalar.activation(squares[0][:], a_ps[0][:], ACT.Square, accum_out=ssq[0][:])
        nc.scalar.activation(msq_first[:], ssq[0][:], ACT.Identity, bias=eps[:], scale=1.0 / J)
        nc.scalar.activation(squares[1][:], a_ps[1][:], ACT.Square, accum_out=ssq[1][:])
        nc.scalar.activation(msq[:], ssq[1][:], ACT.Identity, bias=msq_first[:], scale=1.0 / J)
        a_sb = half_tiles("a_sb")
        for h in range(2):
            nc.scalar.copy(a_sb[h][:], a_ps[h][:])
        nc.gpsimd.tensor_tensor(rinv[:], msq[:], minus_half[:], ALU.pow)
        rinv_sq = sb.tile([P, 1], F32, name="rinv_sq", tag="warm_then_dtab_then_rinv_sq")
        nc.vector.reciprocal(rinv_sq[:], msq[:])

        s_scale, half_scale, out_scale = column("s_scale"), column("half_scale"), column("out_scale")
        silu, silu_m1, tanh = half_tiles("silu"), half_tiles("silu_m1"), half_tiles("tanh")
        nc.scalar.activation(s_scale[:], gain_sb[:], ACT.Identity, scale=rinv[:])
        nc.scalar.activation(silu[0][:], a_ps[0][:], ACT.Silu, scale=s_scale[:])
        nc.scalar.activation(half_scale[:], s_scale[:], ACT.Identity, scale=0.5)
        nc.scalar.activation(silu_m1[0][:], silu[0][:], ACT.Identity, bias=-1.0)
        nc.scalar.activation(tanh[0][:], a_ps[0][:], ACT.Tanh, scale=half_scale[:])
        nc.scalar.activation(silu[1][:], a_ps[1][:], ACT.Silu, scale=s_scale[:])
        nc.scalar.activation(tanh[1][:], a_ps[1][:], ACT.Tanh, scale=half_scale[:])
        nc.scalar.activation(silu_m1[1][:], silu[1][:], ACT.Identity, bias=-1.0)
        nc.gpsimd.tensor_tensor(out_scale[:], og_sb[:], half_scale[:], ALU.mult)

        cross, proj, gated, result = (half_tiles(name) for name in ("cross", "proj", "gated", "result"))
        dot = [column("dot0"), column("dot1")]
        coef = column("coef")
        for h in range(2):
            nc.vector.scalar_tensor_tensor(
                cross[h][:], ta_ps[h][:], 1.0 / J, a_sb[h][:], ALU.mult, ALU.mult, accum_out=dot[h][:]
            )
        nc.vector.tensor_scalar(coef[:], dot[0][:], dot[1][:], rinv_sq[:], ALU.add, ALU.mult)
        gate = [sb.tile([P, HALF], F32, name="gate0", tag="cross1")]
        nc.vector.scalar_tensor_tensor(gate[0][:], tanh[0][:], 1.0, silu_m1[0][:], ALU.subtract, ALU.mult)
        for h in range(2):
            nc.vector.scalar_tensor_tensor(proj[h][:], a_sb[h][:], coef[:], ta_ps[h][:], ALU.mult, ALU.subtract)
        gate.append(sb.tile([P, HALF], F32, name="gate1", tag="a_sb0"))
        nc.vector.scalar_tensor_tensor(gate[1][:], tanh[1][:], 1.0, silu_m1[1][:], ALU.subtract, ALU.mult)
        for h in range(2):
            nc.vector.scalar_tensor_tensor(gated[h][:], gate[h][:], 2.0, proj[h][:], ALU.subtract, ALU.mult)
        for h in range(2):
            nc.vector.scalar_tensor_tensor(
                result[h][:], gated[h][:], out_scale[:], base_sb[:, halves[h]], ALU.mult, ALU.add
            )
            nc.sync.dma_start(out[:, halves[h]], result[h][:])
